import numpy as np
import ml_dtypes

BF16 = ml_dtypes.bfloat16


def bf(x):
    return np.asarray(x, np.float32).astype(BF16)


def f32(x):
    return np.asarray(x, np.float32)


def f64(x):
    return np.asarray(x).astype(np.float64)


def striped(idx):
    return np.tile(idx.reshape(-1, 16).T, (8, 1))


S, K, M, N = 512, 128, 128, 64


def setup_inputs():
    return {"base": bf(np.random.standard_normal((M, S))), "x": bf(np.random.standard_normal((K, N))), "w": bf(np.random.standard_normal((K, M)) / np.sqrt(K)), "b": f32(0.5 * np.random.standard_normal((M, 1))), "offs": striped(np.random.permutation(S)[:N])}


def reference(base, x, w, b, offs):
    idx = offs[:16].T.reshape(-1)
    z = f64(base).copy()
    z[:, idx] = f64(w).T @ f64(x)
    return np.tanh(z + f64(b))

@@ -1,0 +1,44 @@
+import concourse.mybir as mybir
+from concourse.masks import make_identity
+
+P = 128
+S = 512
+N = 64
+
+FLOPS = 2 * P * P * N
+
+BF16, F32, U16 = mybir.dt.bfloat16, mybir.dt.float32, mybir.dt.uint16
+TANH = mybir.ActivationFunctionType.Tanh
+
+
+def tile_scatter_matmul_kernel(tc, base, x, w, b, offs, out):
+    nc = tc.nc
+    with (
+        tc.tile_pool(name="held", bufs=1) as held,
+        tc.psum_pool(name="psum", bufs=1) as psum,
+    ):
+        offsets = held.tile([P, N // 16], U16, name="offsets")
+        nc.sync.dma_start(offsets[:], offs)
+
+        base_tile = held.tile([P, S], BF16, name="base_tile")
+        nc.scalar.dma_start(base_tile[:], base)
+        weights = held.tile([P, P], BF16, name="weights")
+        nc.sync.dma_start(weights[:], w)
+        moving = held.tile([P, N], BF16, name="moving")
+        nc.sync.dma_start(moving[:], x)
+        bias = held.tile([P, 1], F32, name="bias")
+        nc.scalar.dma_start(bias[:], b)
+
+        ident = held.tile([P, P], BF16, name="ident")
+        make_identity(nc, ident[:])
+
+        window = psum.tile([P, S], F32, name="window")
+        nc.tensor.matmul(window[:], ident[:], base_tile[:], start=True, stop=True)
+
+        nc.tensor.matmul(
+            window[:].indirect(offsets[:]), weights[:], moving[:], start=True, stop=True
+        )
+
+        result = held.tile([P, S], F32, name="result")
+        nc.scalar.activation(result[:], window[:], TANH, bias=bias[:])
+        nc.sync.dma_start(out, result[:])

@@ -29,6 +29,10 @@ def tile_scatter_matmul_kernel(tc, base, x, w, b, offs, out):
         bias = held.tile([P, 1], F32, name="bias")
         nc.scalar.dma_start(bias[:], b)
 
+        warm = held.tile([P, 1], F32, name="warm")
+        nc.vector.memset(warm[:], 0.0)
+        nc.scalar.activation(warm[:], warm[:], TANH)
+
         ident = held.tile([P, P], BF16, name="ident")
         make_identity(nc, ident[:])
 

@@ -4,6 +4,7 @@ from concourse.masks import make_identity
 P = 128
 S = 512
 N = 64
+WARM_MATMULS = 3
 
 FLOPS = 2 * P * P * N
 
@@ -29,12 +30,20 @@ def tile_scatter_matmul_kernel(tc, base, x, w, b, offs, out):
         bias = held.tile([P, 1], F32, name="bias")
         nc.scalar.dma_start(bias[:], b)
 
+        zero = held.tile([P, 1], BF16, name="zero")
+        nc.vector.memset(zero[:], 0.0)
         warm = held.tile([P, 1], F32, name="warm")
-        nc.vector.memset(warm[:], 0.0)
-        nc.scalar.activation(warm[:], warm[:], TANH)
+        nc.scalar.activation(warm[:], zero[:], TANH)
 
         ident = held.tile([P, P], BF16, name="ident")
         make_identity(nc, ident[:])
+
+        spare = psum.tile([P, S], F32, name="spare")
+        for i in range(WARM_MATMULS):
+            nc.tensor.matmul(
+                spare[:], zero[:].to_broadcast([P, P]), zero[:].to_broadcast([P, S]),
+                start=True, stop=True,
+            )
 
         window = psum.tile([P, S], F32, name="window")
         nc.tensor.matmul(window[:], ident[:], base_tile[:], start=True, stop=True)

@@ -18,17 +18,16 @@ def tile_scatter_matmul_kernel(tc, base, x, w, b, offs, out):
         tc.tile_pool(name="held", bufs=1) as held,
         tc.psum_pool(name="psum", bufs=1) as psum,
     ):
-        offsets = held.tile([P, N // 16], U16, name="offsets")
-        nc.sync.dma_start(offsets[:], offs)
-
         base_tile = held.tile([P, S], BF16, name="base_tile")
-        nc.scalar.dma_start(base_tile[:], base)
+        nc.sync.dma_start(base_tile[:], base)
         weights = held.tile([P, P], BF16, name="weights")
         nc.sync.dma_start(weights[:], w)
         moving = held.tile([P, N], BF16, name="moving")
         nc.sync.dma_start(moving[:], x)
+        offsets = held.tile([P, N // 16], U16, name="offsets")
+        nc.sync.dma_start(offsets[:], offs)
         bias = held.tile([P, 1], F32, name="bias")
-        nc.scalar.dma_start(bias[:], b)
+        nc.sync.dma_start(bias[:], b)
 
         zero = held.tile([P, 1], BF16, name="zero")
         nc.vector.memset(zero[:], 0.0)

@@ -4,6 +4,7 @@ from concourse.masks import make_identity
 P = 128
 S = 512
 N = 64
+HALF = S // 2
 WARM_MATMULS = 3
 
 FLOPS = 2 * P * P * N
@@ -52,5 +53,7 @@ def tile_scatter_matmul_kernel(tc, base, x, w, b, offs, out):
         )
 
         result = held.tile([P, S], F32, name="result")
-        nc.scalar.activation(result[:], window[:], TANH, bias=bias[:])
-        nc.sync.dma_start(out, result[:])
+        nc.scalar.activation(result[:, 0:HALF], window[:, 0:HALF], TANH, bias=bias[:])
+        nc.sync.dma_start(out[:, 0:HALF], result[:, 0:HALF])
+        nc.scalar.activation(result[:, HALF:S], window[:, HALF:S], TANH, bias=bias[:])
+        nc.scalar.dma_start(out[:, HALF:S], result[:, HALF:S])

@@ -53,7 +53,7 @@ def tile_scatter_matmul_kernel(tc, base, x, w, b, offs, out):
         )
 
         result = held.tile([P, S], F32, name="result")
-        nc.scalar.activation(result[:, 0:HALF], window[:, 0:HALF], TANH, bias=bias[:])
-        nc.sync.dma_start(out[:, 0:HALF], result[:, 0:HALF])
-        nc.scalar.activation(result[:, HALF:S], window[:, HALF:S], TANH, bias=bias[:])
-        nc.scalar.dma_start(out[:, HALF:S], result[:, HALF:S])
+        for first in (0, HALF):
+            columns = slice(first, first + HALF)
+            nc.scalar.activation(result[:, columns], window[:, columns], TANH, bias=bias[:])
+            nc.sync.dma_start(out[:, columns], result[:, columns])

@@ -20,7 +20,8 @@ def tile_scatter_matmul_kernel(tc, base, x, w, b, offs, out):
         tc.psum_pool(name="psum", bufs=1) as psum,
     ):
         base_tile = held.tile([P, S], BF16, name="base_tile")
-        nc.sync.dma_start(base_tile[:], base)
+        for first in (0, HALF):
+            nc.sync.dma_start(base_tile[:, first : first + HALF], base[:, first : first + HALF])
         weights = held.tile([P, P], BF16, name="weights")
         nc.sync.dma_start(weights[:], w)
         moving = held.tile([P, N], BF16, name="moving")
@@ -46,7 +47,11 @@ def tile_scatter_matmul_kernel(tc, base, x, w, b, offs, out):
             )
 
         window = psum.tile([P, S], F32, name="window")
-        nc.tensor.matmul(window[:], ident[:], base_tile[:], start=True, stop=True)
+        for first in (0, HALF):
+            columns = slice(first, first + HALF)
+            nc.tensor.matmul(
+                window[:, columns], ident[:], base_tile[:, columns], start=True, stop=True
+            )
 
         nc.tensor.matmul(
             window[:].indirect(offsets[:]), weights[:], moving[:], start=True, stop=True

@@ -5,7 +5,7 @@ P = 128
 S = 512
 N = 64
 HALF = S // 2
-WARM_MATMULS = 3
+WARM_MATMULS = 2
 
 FLOPS = 2 * P * P * N
 

@@ -5,6 +5,7 @@ P = 128
 S = 512
 N = 64
 HALF = S // 2
+QUARTER = S // 4
 WARM_MATMULS = 2
 
 FLOPS = 2 * P * P * N
@@ -58,7 +59,6 @@ def tile_scatter_matmul_kernel(tc, base, x, w, b, offs, out):
         )
 
         result = held.tile([P, S], F32, name="result")
-        for first in (0, HALF):
-            columns = slice(first, first + HALF)
+        for columns in (slice(0, QUARTER), slice(QUARTER, S)):
             nc.scalar.activation(result[:, columns], window[:, columns], TANH, bias=bias[:])
             nc.sync.dma_start(out[:, columns], result[:, columns])

@@ -5,7 +5,7 @@ P = 128
 S = 512
 N = 64
 HALF = S // 2
-QUARTER = S // 4
+FIRST_PIECE = 3 * S // 8
 WARM_MATMULS = 2
 
 FLOPS = 2 * P * P * N
@@ -59,6 +59,6 @@ def tile_scatter_matmul_kernel(tc, base, x, w, b, offs, out):
         )
 
         result = held.tile([P, S], F32, name="result")
-        for columns in (slice(0, QUARTER), slice(QUARTER, S)):
+        for columns in (slice(0, FIRST_PIECE), slice(FIRST_PIECE, S)):
             nc.scalar.activation(result[:, columns], window[:, columns], TANH, bias=bias[:])
             nc.sync.dma_start(out[:, columns], result[:, columns])

@@ -38,7 +38,8 @@ def tile_scatter_matmul_kernel(tc, base, x, w, b, offs, out):
         nc.scalar.activation(warm[:], zero[:], TANH)
 
         ident = held.tile([P, P], BF16, name="ident")
-        make_identity(nc, ident[:])
+        nc.vector.memset(ident[:], 0.0)
+        make_identity(nc, ident[:], nomemset=True)
 
         spare = psum.tile([P, S], F32, name="spare")
         for i in range(WARM_MATMULS):

@@ -5,6 +5,7 @@ P = 128
 S = 512
 N = 64
 HALF = S // 2
+ROW_ALIGN = 256
 FIRST_PIECE = 3 * S // 8
 WARM_MATMULS = 2
 
@@ -20,16 +21,16 @@ def tile_scatter_matmul_kernel(tc, base, x, w, b, offs, out):
         tc.tile_pool(name="held", bufs=1) as held,
         tc.psum_pool(name="psum", bufs=1) as psum,
     ):
-        base_tile = held.tile([P, S], BF16, name="base_tile")
+        base_tile = held.tile([P, S], BF16, name="base_tile", align_bytes=ROW_ALIGN)
         for first in (0, HALF):
             nc.sync.dma_start(base_tile[:, first : first + HALF], base[:, first : first + HALF])
-        weights = held.tile([P, P], BF16, name="weights")
+        weights = held.tile([P, P], BF16, name="weights", align_bytes=ROW_ALIGN)
         nc.sync.dma_start(weights[:], w)
-        moving = held.tile([P, N], BF16, name="moving")
+        moving = held.tile([P, N], BF16, name="moving", align_bytes=ROW_ALIGN)
         nc.sync.dma_start(moving[:], x)
-        offsets = held.tile([P, N // 16], U16, name="offsets")
+        offsets = held.tile([P, N // 16], U16, name="offsets", align_bytes=ROW_ALIGN)
         nc.sync.dma_start(offsets[:], offs)
-        bias = held.tile([P, 1], F32, name="bias")
+        bias = held.tile([P, 1], F32, name="bias", align_bytes=ROW_ALIGN)
         nc.sync.dma_start(bias[:], b)
 
         zero = held.tile([P, 1], BF16, name="zero")
@@ -59,7 +60,7 @@ def tile_scatter_matmul_kernel(tc, base, x, w, b, offs, out):
             window[:].indirect(offsets[:]), weights[:], moving[:], start=True, stop=True
         )
 
-        result = held.tile([P, S], F32, name="result")
+        result = held.tile([P, S], F32, name="result", align_bytes=ROW_ALIGN)
         for columns in (slice(0, FIRST_PIECE), slice(FIRST_PIECE, S)):
             nc.scalar.activation(result[:, columns], window[:, columns], TANH, bias=bias[:])
             nc.sync.dma_start(out[:, columns], result[:, columns])

import concourse.mybir as mybir
from concourse.masks import make_identity

P = 128
S = 512
N = 64
HALF = S // 2
ROW_ALIGN = 256
FIRST_PIECE = 3 * S // 8
WARM_MATMULS = 2

FLOPS = 2 * P * P * N

BF16, F32, U16 = mybir.dt.bfloat16, mybir.dt.float32, mybir.dt.uint16
TANH = mybir.ActivationFunctionType.Tanh


def tile_scatter_matmul_kernel(tc, base, x, w, b, offs, out):
    nc = tc.nc
    with (
        tc.tile_pool(name="held", bufs=1) as held,
        tc.psum_pool(name="psum", bufs=1) as psum,
    ):
        base_tile = held.tile([P, S], BF16, name="base_tile", align_bytes=ROW_ALIGN)
        for first in (0, HALF):
            nc.sync.dma_start(base_tile[:, first : first + HALF], base[:, first : first + HALF])
        weights = held.tile([P, P], BF16, name="weights", align_bytes=ROW_ALIGN)
        nc.sync.dma_start(weights[:], w)
        moving = held.tile([P, N], BF16, name="moving", align_bytes=ROW_ALIGN)
        nc.sync.dma_start(moving[:], x)
        offsets = held.tile([P, N // 16], U16, name="offsets", align_bytes=ROW_ALIGN)
        nc.sync.dma_start(offsets[:], offs)
        bias = held.tile([P, 1], F32, name="bias", align_bytes=ROW_ALIGN)
        nc.sync.dma_start(bias[:], b)

        zero = held.tile([P, 1], BF16, name="zero")
        nc.vector.memset(zero[:], 0.0)
        warm = held.tile([P, 1], F32, name="warm")
        nc.scalar.activation(warm[:], zero[:], TANH)

        ident = held.tile([P, P], BF16, name="ident")
        nc.vector.memset(ident[:], 0.0)
        make_identity(nc, ident[:], nomemset=True)

        spare = psum.tile([P, S], F32, name="spare")
        for i in range(WARM_MATMULS):
            nc.tensor.matmul(
                spare[:], zero[:].to_broadcast([P, P]), zero[:].to_broadcast([P, S]),
                start=True, stop=True,
            )

        window = psum.tile([P, S], F32, name="window")
        for first in (0, HALF):
            columns = slice(first, first + HALF)
            nc.tensor.matmul(
                window[:, columns], ident[:], base_tile[:, columns], start=True, stop=True
            )

        nc.tensor.matmul(
            window[:].indirect(offsets[:]), weights[:], moving[:], start=True, stop=True
        )

        result = held.tile([P, S], F32, name="result", align_bytes=ROW_ALIGN)
        for columns in (slice(0, FIRST_PIECE), slice(FIRST_PIECE, S)):
            nc.scalar.activation(result[:, columns], window[:, columns], TANH, bias=bias[:])
            nc.sync.dma_start(out[:, columns], result[:, columns])
